import numpy as np
import ml_dtypes


def mxq(x, axis, fmt="e4m3"):
    dtype, down = {"e4m3": (ml_dtypes.float8_e4m3fn, 7), "e5m2": (ml_dtypes.float8_e5m2, 14)}[fmt]
    v = np.moveaxis(np.asarray(x, np.float32).astype(ml_dtypes.bfloat16).astype(np.float64), axis, -1)
    blocks = v.reshape(v.shape[:-1] + (-1, 32))
    amax = np.abs(blocks).max(-1, keepdims=True)
    byte = np.maximum(np.where(amax > 0, np.frexp(amax)[1] - 1 + 127, 0) - down, 1)
    scale = np.exp2(byte - 127.0)
    codes = (blocks / scale).astype(np.float32).astype(dtype).astype(np.float64)
    return np.moveaxis((codes * scale).reshape(v.shape), -1, axis)


WIDE = False


def mx_kscale(k):
    if not WIDE:
        return np.ones(k)
    levels = np.array([10, -10, 5, -5, 0])
    if k % 512:
        return np.exp2(np.random.permutation(np.resize(levels, k // 32))).repeat(32)
    a = np.empty((k // 512, 16))
    for p in range(k // 512):
        a[p, :8] = np.random.permutation(np.resize(levels, 8))
        for g in range(8):
            far = levels[np.abs(levels - a[p, g]) >= 10]
            a[p, g + 8] = far[np.random.randint(len(far))]
    return np.exp2(a.ravel()).repeat(32)


def f64(x):
    return np.asarray(x).astype(np.float64)


def striped(idx):
    return np.tile(idx.reshape(-1, 16).T, (8, 1)).astype(np.uint16)


def unstriped(offs):
    return offs[:16].T.reshape(-1).astype(np.int64)


E2M1 = np.array([0.0, 0.5, 1.0, 1.5, 2.0, 3.0, 4.0, 6.0, -0.0, -0.5, -1.0, -1.5, -2.0, -3.0, -4.0, -6.0])


def pack_weight(w, fmt):
    k, n = w.shape
    w = f64(np.asarray(w, np.float32).astype(ml_dtypes.bfloat16)).reshape(k // 32, 32, n)
    amax = np.abs(w).max(1)
    if fmt == "e4m3":
        byte = np.frexp(amax)[1] - 1 + 127 - 7
    else:
        mant, ex = np.frexp(amax / 6.0)
        byte = np.where(mant > 0.5, ex, ex - 1) + 127
    byte = np.clip(np.where(amax > 0, byte, 1), 1, 254)
    scaled = (w * np.exp2(127.0 - byte)[:, None, :]).reshape(k, n).astype(np.float32)
    by_word = np.ascontiguousarray(scaled.reshape(k // 512, 128, 4, n).transpose(0, 1, 3, 2))
    if fmt == "e4m3":
        words = by_word.astype(ml_dtypes.float8_e4m3fn).view(np.uint8)
    else:
        c = by_word.astype(ml_dtypes.float4_e2m1fn).view(np.uint8) & 0xF
        words = (c[..., 0::2] | (c[..., 1::2] << 4)).reshape(k // 512, 128, 2 * n)
    return np.ascontiguousarray(words), np.ascontiguousarray(byte.astype(np.uint8).reshape(k // 512, 16, n))


def unpack_weight(words, scales, fmt):
    g, _, n = scales.shape
    words = np.ascontiguousarray(words).reshape(g, 128, n, -1)
    if fmt == "e4m3":
        vals = words.view(ml_dtypes.float8_e4m3fn).astype(np.float64)
    else:
        nib = np.empty((g, 128, n, 4), np.uint8)
        nib[..., 0::2] = words & 0xF
        nib[..., 1::2] = words >> 4
        vals = E2M1[nib]
    vals = vals * np.repeat(np.exp2(scales.astype(np.float64) - 127.0), 8, axis=1)[..., None]
    return vals.transpose(0, 1, 3, 2).reshape(g * 512, n)


def gelu(v):
    return 0.5 * v * (1.0 + np.tanh(np.sqrt(2.0 / np.pi) * (v + 0.044715 * v**3)))


def bf(x):
    return np.asarray(x, np.float32).astype(ml_dtypes.bfloat16)

def planes(Y):
    n, m = Y.shape
    b = f64(bf(Y)).reshape(n // 32, 32, m)
    amax = np.abs(b).max(1)
    byte = np.clip(np.where(amax > 0, np.frexp(amax)[1] - 1 + 127 - 7, 1), 1, 254)
    codes = (b * np.exp2(127.0 - byte)[:, None, :]).reshape(n, m).astype(np.float32).astype(ml_dtypes.float8_e4m3fn).view(np.uint8)
    words = codes.reshape(n // 512, 128, 4, m).transpose(0, 1, 3, 2)
    return np.ascontiguousarray(words), np.ascontiguousarray(byte.astype(np.uint8).reshape(n // 512, 16, m))


K, R, N, T, S = 1024, 1024, 512, 2048, 512

def setup_inputs():
    n = np.random.standard_normal
    s = mx_kscale(K)[:, None]
    u = mx_kscale(R)[:, None]
    tab_words, tab_scales = pack_weight(n((K, T)) * s, "e4m3")
    wp_words, wp_scales = pack_weight(n((K, R)) / np.sqrt(K) / s, "e2m1")
    wa = 0.8 * n((K, R)) / np.sqrt(K) / s
    wf = np.exp(0.9 * n((R, N))) / R / u
    return {
        "tab_words": tab_words, "tab_scales": tab_scales,
        "offs": striped(np.random.permutation(T)[:S]),
        "wa": wa.astype(np.float32),
        "wp_words": wp_words, "wp_scales": wp_scales,
        "gain": (np.exp(0.3 * n(R)) * u[:, 0]).astype(np.float32),
        "wf": wf.astype(np.float32),
        "spread": (10.0 * np.exp(0.8 * n(N))).astype(np.float32),
    }

def reference(tab_words, tab_scales, offs, wa, wp_words, wp_scales, gain, wf, spread):
    v = unpack_weight(tab_words, tab_scales, "e4m3")[:, unstriped(offs)]
    wp = unpack_weight(wp_words, wp_scales, "e2m1")
    a = mxq(f64(wa), 0, "e4m3").T @ v
    p = wp.T @ v
    e = np.exp(a) * f64(gain)[:, None]
    q = e * p
    wfq = mxq(f64(wf), 0, "e4m3")
    num = wfq.T @ mxq(q, 0, "e4m3")
    den = wfq.T @ mxq(e, 0, "e4m3")
    y = (num / den) * f64(spread)[:, None]
    words, scales = planes(y)
    return y, words, scales

@@ -1,0 +1,327 @@
+from contextlib import ExitStack
+
+import concourse.mybir as mybir
+
+K, R, N, T, S = 1024, 1024, 512, 2048, 512
+FLOPS = 2 * K * R * S * 2 + 2 * R * N * S * 2
+
+F32 = mybir.dt.float32
+BF16 = mybir.dt.bfloat16
+I32 = mybir.dt.int32
+U32 = mybir.dt.uint32
+U16 = mybir.dt.uint16
+U8 = mybir.dt.uint8
+FP8X4 = mybir.dt.float8_e4m3fn_x4
+FP4X4 = mybir.dt.float4_e2m1fn_x4
+ACT = mybir.ActivationFunctionType
+ALU = mybir.AluOpType
+
+P = 128
+PASS = 512
+HALF = 256
+
+
+def tile_list_station_interpolation_kernel(
+    tc, tab_words, tab_scales, offs, wa, wp_words, wp_scales, gain, wf, spread, out_0, out_1, out_2
+):
+    nc = tc.nc
+    with ExitStack() as ctx:
+        keep = ctx.enter_context(tc.tile_pool(name="keep", bufs=1))
+        reuse = ctx.enter_context(tc.tile_pool(name="reuse", bufs=1))
+        psum = ctx.enter_context(tc.psum_pool(name="psum", bufs=1))
+
+        def sb(name, shape, dtype):
+            return keep.tile(shape, dtype, name=name, align_bytes=64)
+
+        def placed(name, offset, shape, dtype):
+            return reuse.tile(shape, dtype, name=name, offset=offset, align_bytes=64)
+
+        def staged(name, tag, shape, dtype):
+            return keep.tile(shape, dtype, name=name, tag=tag, align_bytes=64)
+
+        def bank(index, name):
+            return psum.tile([P, PASS], F32, name=name, tag="bank%d" % index)
+
+        offsets = keep.tile([P, S // 16], U16, name="offsets")
+        tab_sc = staged("tab_sc", "tab_scales", [P, 2 * T], U8)
+        wp_sc_raw = sb("wp_sc_raw", [P, 2 * R], U8)
+        nc.vector.memset(tab_sc[:, 0:T].bitcast(I32), 0)
+        nc.gpsimd.memset(tab_sc[:, T : 2 * T].bitcast(I32), 0)
+        nc.gpsimd.memset(wp_sc_raw[:].bitcast(I32), 0)
+
+        wa_view = wa.rearrange("(a p j) (b c) -> b a p j c", a=2, j=4, b=2)
+        wf_view = wf.rearrange("(b g t i) n -> b t g i n", b=2, t=4, i=4)
+        tab_w = [sb("tab_w%d" % a, [P, T], U32) for a in range(2)]
+        wa_raw = {(b, a): sb("wa_raw%d%d" % (b, a), [P, 4, PASS], F32) for b in range(2) for a in range(2)}
+        wf_raw = [sb("wf_raw%d" % b, [P, 4, N], F32) for b in range(2)]
+        wp_w_raw = sb("wp_w_raw", [P, 2, PASS], I32)
+        gain_run = sb("gain_run", [P, 2, 16], F32)
+        spread_sb = sb("spread_sb", [P, 4], F32)
+
+        def load_table(a):
+            nc.sync.dma_start(tab_w[a][:].bitcast(I32), tab_words[a].rearrange("p t i -> p (t i)").bitcast(I32))
+
+        def load_wa(b, a):
+            nc.sync.dma_start(wa_raw[b, a][:], wa_view[b, a])
+
+        def load_scale_rows(tile, rows):
+            for quad in range(4):
+                nc.sync.dma_start(
+                    tile[32 * quad : 32 * quad + 4, :].bitcast(I32).rearrange("r (a c) -> r a c", a=2),
+                    rows.bitcast(I32)[:, 4 * quad : 4 * quad + 4, :].rearrange("a r c -> r a c"),
+                )
+
+        gain_view = gain.rearrange("(b g x) -> g b x", b=2, x=16)
+        for i in range(4):
+            nc.sync.dma_start(gain_run[i:P:4, :, 0:13], gain_view[:, :, i : i + 13])
+        load_wa(0, 0)
+        load_scale_rows(tab_sc, tab_scales)
+        nc.sync.dma_start(offsets[:], offs)
+        load_table(0)
+        load_wa(0, 1)
+        load_table(1)
+        load_scale_rows(wp_sc_raw, wp_scales)
+        load_wa(1, 0)
+        nc.sync.dma_start(wp_w_raw[:], wp_words.bitcast(I32).rearrange("a p c -> p a c"))
+        load_wa(1, 1)
+        for b in range(2):
+            for t in range(4):
+                nc.sync.dma_start(wf_raw[b][:, t, :], wf_view[b, t])
+        nc.sync.dma_start(spread_sb[:], spread.rearrange("(p t) -> p t", t=4))
+
+        def copy_on(engine, out, in_):
+            if engine == "scalar":
+                nc.scalar.copy(out, in_)
+            else:
+                nc.vector.tensor_copy(out, in_)
+
+        def shared_copy(out, in_, scalar_share):
+            count = out.shape[1]
+            if scalar_share > 0:
+                copy_on("scalar", out[:, 0:scalar_share], in_[:, 0:scalar_share])
+            if scalar_share < count:
+                copy_on("vector", out[:, scalar_share:count], in_[:, scalar_share:count])
+
+        def quantize(codes, scales, grouped):
+            nc.vector.quantize_mx(out=codes.bitcast(FP8X4), scales=scales, in_=grouped)
+
+        wa_bf = {}
+
+        wa_codes = [{}, {}]
+        wa_sc = [[sb("wa_sc%d%d" % (b, a), [P, PASS], U8) for a in range(2)] for b in range(2)]
+
+        def cast_wa(b, a, scalar_share):
+            wa_bf[b, a] = staged("wa_bf%d%d" % (b, a), "rounded%d%d" % (b, a), [P, 4 * PASS], BF16)
+            shared_copy(
+                wa_bf[b, a][:].rearrange("p (t g i j) -> p g t j i", t=4, i=4, j=4),
+                wa_raw[b, a][:].rearrange("p j (g t i) -> p g t j i", t=4, i=4),
+                scalar_share,
+            )
+
+        def quantize_wa(b, a):
+            wa_codes[b][a] = staged("wa_codes%d%d" % (b, a), "tab_scales" if a + b == 0 else "codes%d%d" % (b, a), [P, PASS], U32)
+            quantize(wa_codes[b][a][:], wa_sc[b][a][:], wa_bf[b, a][:])
+
+        v_w = {}
+        v_sc = [sb("v_sc%d" % a, [P, S], U8) for a in range(2)]
+
+        def gather_scales(a):
+            nc.vector.tensor_copy(v_sc[a][:], tab_sc[:, a * T : (a + 1) * T].indirect(offsets[:]))
+
+        def gather_words(a):
+            v_w[a] = sb("v_w%d" % a, [P, S], U32)
+            nc.vector.tensor_copy(v_w[a][:], tab_w[a][:].indirect(offsets[:]))
+
+        def mx(out, lhsT, lhsT_scale, rhs, rhs_scale, first):
+            nc.tensor.matmul_mx(
+                out=out, lhsT=lhsT, lhsT_scale=lhsT_scale, rhs=rhs.bitcast(FP8X4), rhs_scale=rhs_scale,
+                start=first, stop=not first,
+            )
+
+        def a_pass(banks, b, a):
+            for t in range(4):
+                cols = slice(P * t, P * (t + 1))
+                mx(banks[t][:], wa_codes[b][a][:, cols].bitcast(FP8X4), wa_sc[b][a][:, cols], v_w[a][:], v_sc[a][:], a == 0)
+
+        wp = {}
+
+        def move_wp_words():
+            wp["words"] = sb("wp_w", [P, 4 * R], U8)
+            nc.vector.tensor_copy(
+                wp["words"][:].bitcast(I32).rearrange("p (t g e) -> p g t e", t=4, e=2),
+                wp_w_raw[:].rearrange("p a (g t e) -> p (a g) t e", t=4, e=2),
+            )
+
+        def move_wp_scales():
+            wp["scales"] = sb("wp_sc", [P, 2 * R], U8)
+            nc.vector.tensor_copy(
+                wp["scales"][:].bitcast(I32).rearrange("p (t g) -> p g t", t=4),
+                wp_sc_raw[:].bitcast(I32).rearrange("p (g t) -> p g t", t=4),
+            )
+
+        def p_passes(banks, b):
+            for c in range(4):
+                js = slice(P * c, P * (c + 1))
+                for t in range(4):
+                    for a in range(2):
+                        at = (t * 4 + a * 2 + b) * P
+                        mx(
+                            banks[c][:, P * t : P * (t + 1)],
+                            wp["words"][:, 2 * at : 2 * (at + P)].bitcast(FP4X4), wp["scales"][:, at : at + P],
+                            v_w[a][:, js], v_sc[a][:, js], a == 0,
+                        )
+
+        e32 = [placed("e32_0", 0, [P, 4, S], F32), sb("e32_1", [P, 4, S], F32)]
+        e_bf = [sb("e_bf%d" % b, [P, 4 * S], BF16) for b in range(2)]
+        q_bf = {}
+        e_codes = {1: sb("e_codes1", [P, S], U32)}
+        e_sc = [sb("e_sc%d" % b, [P, S], U8) for b in range(2)]
+        q_codes = [sb("q_codes%d" % b, [P, S], U32) for b in range(2)]
+        q_sc = [sb("q_sc%d" % b, [P, S], U8) for b in range(2)]
+
+        log_gain = sb("log_gain", [P, 2, 4], F32)
+
+        def make_log_gain():
+            gain_sb = sb("gain_sb", [P, 2, 4], F32)
+            rough = sb("rough", [P, 2, 4], F32)
+            inverse = sb("inverse", [P, 2, 4], F32)
+            ratio = sb("ratio", [P, 2, 4], F32)
+            step = sb("step", [P, 2, 4], F32)
+            nc.gpsimd.tensor_copy(gain_sb[:], gain_run[:, :, 0:13:4])
+            nc.scalar.activation(rough[:], gain_sb[:], ACT.Ln)
+            nc.scalar.activation(inverse[:], rough[:], ACT.Exp, scale=-1.0)
+            nc.gpsimd.tensor_tensor(ratio[:], inverse[:], gain_sb[:], ALU.mult)
+            nc.gpsimd.tensor_scalar(step[:], ratio[:], 1.0, -1.0, ALU.mult, ALU.add)
+            nc.gpsimd.tensor_tensor(log_gain[:], step[:], rough[:], ALU.add)
+
+        def exps(banks, b):
+            for t in range(4):
+                nc.scalar.activation(e32[b][:, t, :], banks[t][:], ACT.Exp, bias=log_gain[:, b, t : t + 1])
+
+        def round_e(b, js, scalar_share):
+            shared_copy(
+                e_bf[b][:, 4 * js.start : 4 * js.stop].rearrange("p (c i t) -> p c t i", i=4, t=4),
+                e32[b][:, :, js].rearrange("p t (c i) -> p c t i", i=4),
+                scalar_share,
+            )
+
+        def make_q(banks, b, c):
+            nc.vector.tensor_tensor(
+                q_bf[b][:, 4 * P * c : 4 * P * (c + 1)].rearrange("p (c i t) -> p c t i", i=4, t=4),
+                banks[c][:].rearrange("p (t c i) -> p c t i", t=4, i=4),
+                e32[b][:, :, P * c : P * (c + 1)].rearrange("p t (c i) -> p c t i", i=4),
+                ALU.mult,
+            )
+
+        wf_bf = {}
+        wf_codes = [sb("wf_codes%d" % b, [P, N], U32) for b in range(2)]
+        wf_sc = [sb("wf_sc%d" % b, [P, N], U8) for b in range(2)]
+
+        def cast_wf(b, scalar_share):
+            wf_bf[b] = staged("wf_bf1", "rounded_wf1", [P, 4 * N], BF16) if b else placed("wf_bf0", 0, [P, 4 * N], BF16)
+            shared_copy(
+                wf_bf[b][:].rearrange("p (u m j) -> p m j u", u=4, j=4),
+                wf_raw[b][:].rearrange("p j (m u) -> p m j u", u=4),
+                scalar_share,
+            )
+
+        def quantize_wf(b):
+            quantize(wf_codes[b][:], wf_sc[b][:], wf_bf[b][:])
+
+        def second(out, u, codes, scales, js):
+            cols = slice(P * u, P * (u + 1))
+            for b in range(2):
+                mx(out, wf_codes[b][:, cols].bitcast(FP8X4), wf_sc[b][:, cols], codes[b][:, js], scales[b][:, js], b == 0)
+
+        halves = [slice(0, HALF), slice(HALF, S)]
+        make_log_gain()
+        cast_wa(0, 0, 32)
+        gather_scales(0)
+        gather_scales(1)
+        gather_words(0)
+        quantize_wa(0, 0)
+        a_banks = [bank(t, "a0_%d" % t) for t in range(4)]
+        a_pass(a_banks, 0, 0)
+        cast_wa(0, 1, 20)
+        quantize_wa(0, 1)
+        gather_words(1)
+        a_pass(a_banks, 0, 1)
+        move_wp_scales()
+        exps(a_banks, 0)
+        cast_wa(1, 0, 0)
+        move_wp_words()
+        quantize_wa(1, 0)
+        cast_wa(1, 1, 0)
+        quantize_wa(1, 1)
+        a_banks = [bank(t, "a1_%d" % t) for t in range(4)]
+        a_pass(a_banks, 1, 0)
+        a_pass(a_banks, 1, 1)
+        exps(a_banks, 1)
+        p_banks = [bank(4 + c, "p0_%d" % c) for c in range(4)]
+        p_passes(p_banks, 0)
+        round_e(0, halves[0], 64)
+        round_e(0, halves[1], 64)
+        q_bf[0] = staged("q_bf0", "rounded11", [P, 4 * S], BF16)
+        for c in range(4):
+            make_q(p_banks, 0, c)
+        p_banks = [bank(4 + c, "p1_%d" % c) for c in range(4)]
+        p_passes(p_banks, 1)
+        cast_wf(0, 0)
+        e_codes[0] = placed("e_codes0", 4096, [P, S], U32)
+        quantize(e_codes[0][:], e_sc[0][:], e_bf[0][:])
+        quantize_wf(0)
+        cast_wf(1, 40)
+        round_e(1, halves[0], 64)
+        quantize_wf(1)
+        q_bf[1] = staged("q_bf1", "rounded_wf1", [P, 4 * S], BF16)
+
+        root = sb("root", [P, 2, 4, HALF], F32)
+        inv_den = sb("inv_den", [P, 2, 4, HALF], F32)
+        for h in range(2):
+            js = halves[h]
+            if h == 1:
+                round_e(1, js, 0)
+            quantize(e_codes[1][:, js], e_sc[1][:, js], e_bf[1][:, 4 * js.start : 4 * js.stop])
+            for k in range(2):
+                den = bank(2 * h + k, "den%d%d" % (h, k))
+                for u in (2 * k, 2 * k + 1):
+                    second(den[:, HALF * (u % 2) : HALF * (u % 2 + 1)], u, e_codes, e_sc, js)
+                pair = slice(2 * k, 2 * k + 2)
+                nc.scalar.activation(root[:, h, pair, :].rearrange("p u j -> p (u j)"), den[:], ACT.Abs_reciprocal_sqrt)
+                nc.scalar.activation(inv_den[:, h, pair, :], root[:, h, pair, :], ACT.Square)
+        quantize(q_codes[0][:], q_sc[0][:], q_bf[0][:])
+
+        y_sc = sb("y_sc", [P, S], U8)
+        out_rows = out_0.rearrange("(p u) j -> p u j", u=4)
+        out_words = out_1[0].rearrange("p m t -> p (m t)").bitcast(I32)
+        num_banks = []
+        for h in range(2):
+            js = slice(HALF * h, HALF * (h + 1))
+            make_q(p_banks, 1, 2 * h)
+            make_q(p_banks, 1, 2 * h + 1)
+            quantize(q_codes[1][:, js], q_sc[1][:, js], q_bf[1][:, 4 * HALF * h : 4 * HALF * (h + 1)])
+            pair = [bank(4 + 2 * h + k, "num%d%d" % (h, k)) for k in range(2)]
+            num_banks.append(pair)
+            for u in range(4):
+                second(pair[u // 2][:, HALF * (u % 2) : HALF * (u % 2 + 1)], u, q_codes, q_sc, js)
+        for h in range(2):
+            js = slice(HALF * h, HALF * (h + 1))
+            y32 = sb("y32_%d" % h, [P, 4, HALF], F32)
+            y_bf = sb("y_bf%d" % h, [P, 4 * HALF], BF16)
+            y_codes = sb("y_codes%d" % h, [P, HALF], U32)
+            for u in range(4):
+                nc.vector.scalar_tensor_tensor(
+                    y32[:, u, :], num_banks[h][u // 2][:, HALF * (u % 2) : HALF * (u % 2 + 1)],
+                    spread_sb[:, u : u + 1], inv_den[:, h, u, :], ALU.mult, ALU.mult,
+                )
+            nc.sync.dma_start(out_rows[:, :, js], y32[:])
+            shared_copy(
+                y_bf[:].rearrange("p (c i u) -> p c u i", i=4, u=4),
+                y32[:].rearrange("p u (c i) -> p c u i", i=4),
+                64 if h == 0 else 20,
+            )
+            quantize(y_codes[:], y_sc[:, js], y_bf[:])
+            nc.sync.dma_start(out_words[:, js], y_codes[:].bitcast(I32))
+        for quad in range(4):
+            queue = nc.scalar if quad % 2 else nc.sync
+            queue.dma_start(out_2[0, 4 * quad : 4 * quad + 4, :].bitcast(I32), y_sc[32 * quad : 32 * quad + 4, :].bitcast(I32))

@@ -78,11 +78,11 @@ def tile_list_station_interpolation_kernel(
         load_scale_rows(tab_sc, tab_scales)
         nc.sync.dma_start(offsets[:], offs)
         load_table(0)
-        load_wa(0, 1)
         load_table(1)
+        load_wa(0, 1)
         load_scale_rows(wp_sc_raw, wp_scales)
-        load_wa(1, 0)
         nc.sync.dma_start(wp_w_raw[:], wp_words.bitcast(I32).rearrange("a p c -> p a c"))
+        load_wa(1, 0)
         load_wa(1, 1)
         for b in range(2):
             for t in range(4):
@@ -110,17 +110,21 @@ def tile_list_station_interpolation_kernel(
         wa_codes = [{}, {}]
         wa_sc = [[sb("wa_sc%d%d" % (b, a), [P, PASS], U8) for a in range(2)] for b in range(2)]
 
-        def cast_wa(b, a, scalar_share):
-            wa_bf[b, a] = staged("wa_bf%d%d" % (b, a), "rounded%d%d" % (b, a), [P, 4 * PASS], BF16)
-            shared_copy(
-                wa_bf[b, a][:].rearrange("p (t g i j) -> p g t j i", t=4, i=4, j=4),
-                wa_raw[b, a][:].rearrange("p j (g t i) -> p g t j i", t=4, i=4),
-                scalar_share,
+        def cast_wa(b, a, t, engine):
+            if t == 0:
+                wa_bf[b, a] = staged("wa_bf%d%d" % (b, a), "rounded%d%d" % (b, a), [P, 4 * PASS], BF16)
+            copy_on(
+                engine,
+                wa_bf[b, a][:].rearrange("p (t g h i j) -> p t g h j i", t=4, h=2, i=2, j=4)[:, t],
+                wa_raw[b, a][:].rearrange("p j (g t h i) -> p t g h j i", t=4, h=2, i=2)[:, t],
             )
 
-        def quantize_wa(b, a):
-            wa_codes[b][a] = staged("wa_codes%d%d" % (b, a), "tab_scales" if a + b == 0 else "codes%d%d" % (b, a), [P, PASS], U32)
-            quantize(wa_codes[b][a][:], wa_sc[b][a][:], wa_bf[b, a][:])
+        def quantize_wa(b, a, first, count):
+            if first == 0:
+                tag = "tab_scales" if a + b == 0 else "codes%d%d" % (b, a)
+                wa_codes[b][a] = staged("wa_codes%d%d" % (b, a), tag, [P, PASS], U32)
+            cols = slice(P * first, P * (first + count))
+            quantize(wa_codes[b][a][:, cols], wa_sc[b][a][:, cols], wa_bf[b, a][:, 4 * cols.start : 4 * cols.stop])
 
         v_w = {}
         v_sc = [sb("v_sc%d" % a, [P, S], U8) for a in range(2)]
@@ -200,16 +204,16 @@ def tile_list_station_interpolation_kernel(
 
         def round_e(b, js, scalar_share):
             shared_copy(
-                e_bf[b][:, 4 * js.start : 4 * js.stop].rearrange("p (c i t) -> p c t i", i=4, t=4),
-                e32[b][:, :, js].rearrange("p t (c i) -> p c t i", i=4),
+                e_bf[b][:, 4 * js.start : 4 * js.stop].rearrange("p (c i t) -> p c t i", i=2, t=4),
+                e32[b][:, :, js].rearrange("p t (c i) -> p c t i", i=2),
                 scalar_share,
             )
 
         def make_q(banks, b, c):
             nc.vector.tensor_tensor(
-                q_bf[b][:, 4 * P * c : 4 * P * (c + 1)].rearrange("p (c i t) -> p c t i", i=4, t=4),
-                banks[c][:].rearrange("p (t c i) -> p c t i", t=4, i=4),
-                e32[b][:, :, P * c : P * (c + 1)].rearrange("p t (c i) -> p c t i", i=4),
+                q_bf[b][:, 4 * P * c : 4 * P * (c + 1)].rearrange("p (c i t) -> p c t i", i=2, t=4),
+                banks[c][:].rearrange("p (t c i) -> p c t i", t=4, i=2),
+                e32[b][:, :, P * c : P * (c + 1)].rearrange("p t (c i) -> p c t i", i=2),
                 ALU.mult,
             )
 
@@ -217,13 +221,14 @@ def tile_list_station_interpolation_kernel(
         wf_codes = [sb("wf_codes%d" % b, [P, N], U32) for b in range(2)]
         wf_sc = [sb("wf_sc%d" % b, [P, N], U8) for b in range(2)]
 
-        def cast_wf(b, scalar_share):
+        def cast_wf(b, engines):
             wf_bf[b] = staged("wf_bf1", "rounded_wf1", [P, 4 * N], BF16) if b else placed("wf_bf0", 0, [P, 4 * N], BF16)
-            shared_copy(
-                wf_bf[b][:].rearrange("p (u m j) -> p m j u", u=4, j=4),
-                wf_raw[b][:].rearrange("p j (m u) -> p m j u", u=4),
-                scalar_share,
-            )
+            for w in range(2):
+                copy_on(
+                    engines[w],
+                    wf_bf[b][:].rearrange("p (w u m j) -> p w m j u", w=2, u=2, j=4)[:, w],
+                    wf_raw[b][:].rearrange("p j (m w u) -> p w m j u", w=2, u=2)[:, w],
+                )
 
         def quantize_wf(b):
             quantize(wf_codes[b][:], wf_sc[b][:], wf_bf[b][:])
@@ -235,43 +240,47 @@ def tile_list_station_interpolation_kernel(
 
         halves = [slice(0, HALF), slice(HALF, S)]
         make_log_gain()
-        cast_wa(0, 0, 32)
+        for t in range(4):
+            cast_wa(0, 0, t, "scalar")
         gather_scales(0)
         gather_scales(1)
         gather_words(0)
-        quantize_wa(0, 0)
+        quantize_wa(0, 0, 0, 4)
         a_banks = [bank(t, "a0_%d" % t) for t in range(4)]
         a_pass(a_banks, 0, 0)
-        cast_wa(0, 1, 20)
-        quantize_wa(0, 1)
         gather_words(1)
+        for t in range(4):
+            cast_wa(0, 1, t, "vector" if t < 2 else "scalar")
+            quantize_wa(0, 1, t, 1)
         a_pass(a_banks, 0, 1)
-        move_wp_scales()
         exps(a_banks, 0)
-        cast_wa(1, 0, 0)
+        move_wp_scales()
         move_wp_words()
-        quantize_wa(1, 0)
-        cast_wa(1, 1, 0)
-        quantize_wa(1, 1)
+        for t in range(4):
+            cast_wa(1, 0, t, "vector")
+        quantize_wa(1, 0, 0, 4)
+        for t in range(4):
+            cast_wa(1, 1, t, "vector" if t < 3 else "scalar")
+            quantize_wa(1, 1, t, 1)
         a_banks = [bank(t, "a1_%d" % t) for t in range(4)]
         a_pass(a_banks, 1, 0)
         a_pass(a_banks, 1, 1)
         exps(a_banks, 1)
         p_banks = [bank(4 + c, "p0_%d" % c) for c in range(4)]
         p_passes(p_banks, 0)
-        round_e(0, halves[0], 64)
-        round_e(0, halves[1], 64)
+        round_e(0, halves[0], 128)
+        round_e(0, halves[1], 128)
         q_bf[0] = staged("q_bf0", "rounded11", [P, 4 * S], BF16)
         for c in range(4):
             make_q(p_banks, 0, c)
         p_banks = [bank(4 + c, "p1_%d" % c) for c in range(4)]
         p_passes(p_banks, 1)
-        cast_wf(0, 0)
+        cast_wf(0, ("vector", "vector"))
         e_codes[0] = placed("e_codes0", 4096, [P, S], U32)
         quantize(e_codes[0][:], e_sc[0][:], e_bf[0][:])
         quantize_wf(0)
-        cast_wf(1, 40)
-        round_e(1, halves[0], 64)
+        round_e(1, halves[0], 128)
+        cast_wf(1, ("scalar", "vector"))
         quantize_wf(1)
         q_bf[1] = staged("q_bf1", "rounded_wf1", [P, 4 * S], BF16)
 
@@ -280,7 +289,7 @@ def tile_list_station_interpolation_kernel(
         for h in range(2):
             js = halves[h]
             if h == 1:
-                round_e(1, js, 0)
+                round_e(1, js, 128)
             quantize(e_codes[1][:, js], e_sc[1][:, js], e_bf[1][:, 4 * js.start : 4 * js.stop])
             for k in range(2):
                 den = bank(2 * h + k, "den%d%d" % (h, k))
@@ -316,9 +325,9 @@ def tile_list_station_interpolation_kernel(
                 )
             nc.sync.dma_start(out_rows[:, :, js], y32[:])
             shared_copy(
-                y_bf[:].rearrange("p (c i u) -> p c u i", i=4, u=4),
-                y32[:].rearrange("p u (c i) -> p c u i", i=4),
-                64 if h == 0 else 20,
+                y_bf[:].rearrange("p (c i u) -> p c u i", i=2, u=4),
+                y32[:].rearrange("p u (c i) -> p c u i", i=2),
+                128 if h == 0 else 40,
             )
             quantize(y_codes[:], y_sc[:, js], y_bf[:])
             nc.sync.dma_start(out_words[:, js], y_codes[:].bitcast(I32))

@@ -47,6 +47,8 @@ def tile_list_station_interpolation_kernel(
         wp_sc_raw = sb("wp_sc_raw", [P, 2 * R], U8)
         nc.vector.memset(tab_sc[:, 0:T].bitcast(I32), 0)
         nc.gpsimd.memset(tab_sc[:, T : 2 * T].bitcast(I32), 0)
+        v_sc = sb("v_sc", [P, 2 * S], U8)
+        nc.vector.memset(v_sc[:].bitcast(I32), 0)
         nc.gpsimd.memset(wp_sc_raw[:].bitcast(I32), 0)
 
         wa_view = wa.rearrange("(a p j) (b c) -> b a p j c", a=2, j=4, b=2)
@@ -64,30 +66,18 @@ def tile_list_station_interpolation_kernel(
         def load_wa(b, a):
             nc.sync.dma_start(wa_raw[b, a][:], wa_view[b, a])
 
-        def load_scale_rows(tile, rows):
-            for quad in range(4):
-                nc.sync.dma_start(
-                    tile[32 * quad : 32 * quad + 4, :].bitcast(I32).rearrange("r (a c) -> r a c", a=2),
-                    rows.bitcast(I32)[:, 4 * quad : 4 * quad + 4, :].rearrange("a r c -> r a c"),
-                )
 
         gain_view = gain.rearrange("(b g x) -> g b x", b=2, x=16)
         for i in range(4):
             nc.sync.dma_start(gain_run[i:P:4, :, 0:13], gain_view[:, :, i : i + 13])
-        load_wa(0, 0)
-        load_scale_rows(tab_sc, tab_scales)
+        nc.sync.dma_start(
+            tab_sc[0:P:8, :].bitcast(I32).rearrange("q (a c) -> q a c", a=2),
+            tab_scales.bitcast(I32).rearrange("a q c -> q a c"),
+        )
         nc.sync.dma_start(offsets[:], offs)
+        load_wa(0, 0)
         load_table(0)
         load_table(1)
-        load_wa(0, 1)
-        load_scale_rows(wp_sc_raw, wp_scales)
-        nc.sync.dma_start(wp_w_raw[:], wp_words.bitcast(I32).rearrange("a p c -> p a c"))
-        load_wa(1, 0)
-        load_wa(1, 1)
-        for b in range(2):
-            for t in range(4):
-                nc.sync.dma_start(wf_raw[b][:, t, :], wf_view[b, t])
-        nc.sync.dma_start(spread_sb[:], spread.rearrange("(p t) -> p t", t=4))
 
         def copy_on(engine, out, in_):
             if engine == "scalar":
@@ -127,10 +117,14 @@ def tile_list_station_interpolation_kernel(
             quantize(wa_codes[b][a][:, cols], wa_sc[b][a][:, cols], wa_bf[b, a][:, 4 * cols.start : 4 * cols.stop])
 
         v_w = {}
-        v_sc = [sb("v_sc%d" % a, [P, S], U8) for a in range(2)]
+        picked_sc = sb("picked_sc", [P, 2 * S], U8)
 
         def gather_scales(a):
-            nc.vector.tensor_copy(v_sc[a][:], tab_sc[:, a * T : (a + 1) * T].indirect(offsets[:]))
+            nc.vector.tensor_copy(picked_sc[:, a * S : (a + 1) * S], tab_sc[:, a * T : (a + 1) * T].indirect(offsets[:]))
+
+        def move_scale_rows():
+            for r in range(4):
+                nc.sync.dma_start(v_sc[r:P:32, :].bitcast(I32), picked_sc[8 * r : P : 32, :].bitcast(I32))
 
         def gather_words(a):
             v_w[a] = sb("v_w%d" % a, [P, S], U32)
@@ -145,7 +139,7 @@ def tile_list_station_interpolation_kernel(
         def a_pass(banks, b, a):
             for t in range(4):
                 cols = slice(P * t, P * (t + 1))
-                mx(banks[t][:], wa_codes[b][a][:, cols].bitcast(FP8X4), wa_sc[b][a][:, cols], v_w[a][:], v_sc[a][:], a == 0)
+                mx(banks[t][:], wa_codes[b][a][:, cols].bitcast(FP8X4), wa_sc[b][a][:, cols], v_w[a][:], v_sc[:, a * S : (a + 1) * S], a == 0)
 
         wp = {}
 
@@ -172,7 +166,7 @@ def tile_list_station_interpolation_kernel(
                         mx(
                             banks[c][:, P * t : P * (t + 1)],
                             wp["words"][:, 2 * at : 2 * (at + P)].bitcast(FP4X4), wp["scales"][:, at : at + P],
-                            v_w[a][:, js], v_sc[a][:, js], a == 0,
+                            v_w[a][:, js], v_sc[:, a * S + js.start : a * S + js.stop], a == 0,
                         )
 
         e32 = [placed("e32_0", 0, [P, 4, S], F32), sb("e32_1", [P, 4, S], F32)]
@@ -238,12 +232,29 @@ def tile_list_station_interpolation_kernel(
             for b in range(2):
                 mx(out, wf_codes[b][:, cols].bitcast(FP8X4), wf_sc[b][:, cols], codes[b][:, js], scales[b][:, js], b == 0)
 
+        def load_the_rest():
+            load_wa(0, 1)
+            for r in range(4):
+                nc.sync.dma_start(
+                    wp_sc_raw[r:P:32, :].bitcast(I32).rearrange("q (a c) -> q a c", a=2),
+                    wp_scales.bitcast(I32)[:, r:16:4, :].rearrange("a q c -> q a c"),
+                )
+            nc.sync.dma_start(wp_w_raw[:], wp_words.bitcast(I32).rearrange("a p c -> p a c"))
+            load_wa(1, 0)
+            load_wa(1, 1)
+            for b in range(2):
+                for t in range(4):
+                    nc.sync.dma_start(wf_raw[b][:, t, :], wf_view[b, t])
+            nc.sync.dma_start(spread_sb[:], spread.rearrange("(p t) -> p t", t=4))
+
         halves = [slice(0, HALF), slice(HALF, S)]
         make_log_gain()
         for t in range(4):
             cast_wa(0, 0, t, "scalar")
         gather_scales(0)
         gather_scales(1)
+        move_scale_rows()
+        load_the_rest()
         gather_words(0)
         quantize_wa(0, 0, 0, 4)
         a_banks = [bank(t, "a0_%d" % t) for t in range(4)]
@@ -331,6 +342,6 @@ def tile_list_station_interpolation_kernel(
             )
             quantize(y_codes[:], y_sc[:, js], y_bf[:])
             nc.sync.dma_start(out_words[:, js], y_codes[:].bitcast(I32))
-        for quad in range(4):
-            queue = nc.scalar if quad % 2 else nc.sync
-            queue.dma_start(out_2[0, 4 * quad : 4 * quad + 4, :].bitcast(I32), y_sc[32 * quad : 32 * quad + 4, :].bitcast(I32))
+        for r in range(4):
+            queue = nc.sync if r % 2 else nc.scalar
+            queue.dma_start(out_2[0, r:16:4, :].bitcast(I32), y_sc[r:P:32, :].bitcast(I32))

@@ -67,16 +67,16 @@ def tile_list_station_interpolation_kernel(
             nc.sync.dma_start(wa_raw[b, a][:], wa_view[b, a])
 
 
-        gain_view = gain.rearrange("(b g x) -> g b x", b=2, x=16)
-        for i in range(4):
-            nc.sync.dma_start(gain_run[i:P:4, :, 0:13], gain_view[:, :, i : i + 13])
+        nc.sync.dma_start(offsets[:], offs)
+        load_wa(0, 0)
         nc.sync.dma_start(
             tab_sc[0:P:8, :].bitcast(I32).rearrange("q (a c) -> q a c", a=2),
             tab_scales.bitcast(I32).rearrange("a q c -> q a c"),
         )
-        nc.sync.dma_start(offsets[:], offs)
-        load_wa(0, 0)
         load_table(0)
+        gain_view = gain.rearrange("(b g x) -> g b x", b=2, x=16)
+        for i in range(4):
+            nc.sync.dma_start(gain_run[i:P:4, :, 0:13], gain_view[:, :, i : i + 13])
         load_table(1)
 
         def copy_on(engine, out, in_):
@@ -248,9 +248,9 @@ def tile_list_station_interpolation_kernel(
             nc.sync.dma_start(spread_sb[:], spread.rearrange("(p t) -> p t", t=4))
 
         halves = [slice(0, HALF), slice(HALF, S)]
-        make_log_gain()
         for t in range(4):
             cast_wa(0, 0, t, "scalar")
+        make_log_gain()
         gather_scales(0)
         gather_scales(1)
         move_scale_rows()
@@ -334,7 +334,10 @@ def tile_list_station_interpolation_kernel(
                     y32[:, u, :], num_banks[h][u // 2][:, HALF * (u % 2) : HALF * (u % 2 + 1)],
                     spread_sb[:, u : u + 1], inv_den[:, h, u, :], ALU.mult, ALU.mult,
                 )
-            nc.sync.dma_start(out_rows[:, :, js], y32[:])
+                if h == 1 and u % 2 == 1:
+                    nc.sync.dma_start(out_rows[:, u - 1 : u + 1, js], y32[:, u - 1 : u + 1, :])
+            if h == 0:
+                nc.sync.dma_start(out_rows[:, :, js], y32[:])
             shared_copy(
                 y_bf[:].rearrange("p (c i u) -> p c u i", i=2, u=4),
                 y32[:].rearrange("p u (c i) -> p c u i", i=2),

from contextlib import ExitStack

import concourse.mybir as mybir

K, R, N, T, S = 1024, 1024, 512, 2048, 512
FLOPS = 2 * K * R * S * 2 + 2 * R * N * S * 2

F32 = mybir.dt.float32
BF16 = mybir.dt.bfloat16
I32 = mybir.dt.int32
U32 = mybir.dt.uint32
U16 = mybir.dt.uint16
U8 = mybir.dt.uint8
FP8X4 = mybir.dt.float8_e4m3fn_x4
FP4X4 = mybir.dt.float4_e2m1fn_x4
ACT = mybir.ActivationFunctionType
ALU = mybir.AluOpType

P = 128
PASS = 512
HALF = 256


def tile_list_station_interpolation_kernel(
    tc, tab_words, tab_scales, offs, wa, wp_words, wp_scales, gain, wf, spread, out_0, out_1, out_2
):
    nc = tc.nc
    with ExitStack() as ctx:
        keep = ctx.enter_context(tc.tile_pool(name="keep", bufs=1))
        reuse = ctx.enter_context(tc.tile_pool(name="reuse", bufs=1))
        psum = ctx.enter_context(tc.psum_pool(name="psum", bufs=1))

        def sb(name, shape, dtype):
            return keep.tile(shape, dtype, name=name, align_bytes=64)

        def placed(name, offset, shape, dtype):
            return reuse.tile(shape, dtype, name=name, offset=offset, align_bytes=64)

        def staged(name, tag, shape, dtype):
            return keep.tile(shape, dtype, name=name, tag=tag, align_bytes=64)

        def bank(index, name):
            return psum.tile([P, PASS], F32, name=name, tag="bank%d" % index)

        offsets = keep.tile([P, S // 16], U16, name="offsets")
        tab_sc = staged("tab_sc", "tab_scales", [P, 2 * T], U8)
        wp_sc_raw = sb("wp_sc_raw", [P, 2 * R], U8)
        nc.vector.memset(tab_sc[:, 0:T].bitcast(I32), 0)
        nc.gpsimd.memset(tab_sc[:, T : 2 * T].bitcast(I32), 0)
        v_sc = sb("v_sc", [P, 2 * S], U8)
        nc.vector.memset(v_sc[:].bitcast(I32), 0)
        nc.gpsimd.memset(wp_sc_raw[:].bitcast(I32), 0)

        wa_view = wa.rearrange("(a p j) (b c) -> b a p j c", a=2, j=4, b=2)
        wf_view = wf.rearrange("(b g t i) n -> b t g i n", b=2, t=4, i=4)
        tab_w = [sb("tab_w%d" % a, [P, T], U32) for a in range(2)]
        wa_raw = {(b, a): sb("wa_raw%d%d" % (b, a), [P, 4, PASS], F32) for b in range(2) for a in range(2)}
        wf_raw = [sb("wf_raw%d" % b, [P, 4, N], F32) for b in range(2)]
        wp_w_raw = sb("wp_w_raw", [P, 2, PASS], I32)
        gain_run = sb("gain_run", [P, 2, 16], F32)
        spread_sb = sb("spread_sb", [P, 4], F32)

        def load_table(a):
            nc.sync.dma_start(tab_w[a][:].bitcast(I32), tab_words[a].rearrange("p t i -> p (t i)").bitcast(I32))

        def load_wa(b, a):
            nc.sync.dma_start(wa_raw[b, a][:], wa_view[b, a])


        nc.sync.dma_start(offsets[:], offs)
        load_wa(0, 0)
        nc.sync.dma_start(
            tab_sc[0:P:8, :].bitcast(I32).rearrange("q (a c) -> q a c", a=2),
            tab_scales.bitcast(I32).rearrange("a q c -> q a c"),
        )
        load_table(0)
        gain_view = gain.rearrange("(b g x) -> g b x", b=2, x=16)
        for i in range(4):
            nc.sync.dma_start(gain_run[i:P:4, :, 0:13], gain_view[:, :, i : i + 13])
        load_table(1)

        def copy_on(engine, out, in_):
            if engine == "scalar":
                nc.scalar.copy(out, in_)
            else:
                nc.vector.tensor_copy(out, in_)

        def shared_copy(out, in_, scalar_share):
            count = out.shape[1]
            if scalar_share > 0:
                copy_on("scalar", out[:, 0:scalar_share], in_[:, 0:scalar_share])
            if scalar_share < count:
                copy_on("vector", out[:, scalar_share:count], in_[:, scalar_share:count])

        def quantize(codes, scales, grouped):
            nc.vector.quantize_mx(out=codes.bitcast(FP8X4), scales=scales, in_=grouped)

        wa_bf = {}

        wa_codes = [{}, {}]
        wa_sc = [[sb("wa_sc%d%d" % (b, a), [P, PASS], U8) for a in range(2)] for b in range(2)]

        def cast_wa(b, a, t, engine):
            if t == 0:
                wa_bf[b, a] = staged("wa_bf%d%d" % (b, a), "rounded%d%d" % (b, a), [P, 4 * PASS], BF16)
            copy_on(
                engine,
                wa_bf[b, a][:].rearrange("p (t g h i j) -> p t g h j i", t=4, h=2, i=2, j=4)[:, t],
                wa_raw[b, a][:].rearrange("p j (g t h i) -> p t g h j i", t=4, h=2, i=2)[:, t],
            )

        def quantize_wa(b, a, first, count):
            if first == 0:
                tag = "tab_scales" if a + b == 0 else "codes%d%d" % (b, a)
                wa_codes[b][a] = staged("wa_codes%d%d" % (b, a), tag, [P, PASS], U32)
            cols = slice(P * first, P * (first + count))
            quantize(wa_codes[b][a][:, cols], wa_sc[b][a][:, cols], wa_bf[b, a][:, 4 * cols.start : 4 * cols.stop])

        v_w = {}
        picked_sc = sb("picked_sc", [P, 2 * S], U8)

        def gather_scales(a):
            nc.vector.tensor_copy(picked_sc[:, a * S : (a + 1) * S], tab_sc[:, a * T : (a + 1) * T].indirect(offsets[:]))

        def move_scale_rows():
            for r in range(4):
                nc.sync.dma_start(v_sc[r:P:32, :].bitcast(I32), picked_sc[8 * r : P : 32, :].bitcast(I32))

        def gather_words(a):
            v_w[a] = sb("v_w%d" % a, [P, S], U32)
            nc.vector.tensor_copy(v_w[a][:], tab_w[a][:].indirect(offsets[:]))

        def mx(out, lhsT, lhsT_scale, rhs, rhs_scale, first):
            nc.tensor.matmul_mx(
                out=out, lhsT=lhsT, lhsT_scale=lhsT_scale, rhs=rhs.bitcast(FP8X4), rhs_scale=rhs_scale,
                start=first, stop=not first,
            )

        def a_pass(banks, b, a):
            for t in range(4):
                cols = slice(P * t, P * (t + 1))
                mx(banks[t][:], wa_codes[b][a][:, cols].bitcast(FP8X4), wa_sc[b][a][:, cols], v_w[a][:], v_sc[:, a * S : (a + 1) * S], a == 0)

        wp = {}

        def move_wp_words():
            wp["words"] = sb("wp_w", [P, 4 * R], U8)
            nc.vector.tensor_copy(
                wp["words"][:].bitcast(I32).rearrange("p (t g e) -> p g t e", t=4, e=2),
                wp_w_raw[:].rearrange("p a (g t e) -> p (a g) t e", t=4, e=2),
            )

        def move_wp_scales():
            wp["scales"] = sb("wp_sc", [P, 2 * R], U8)
            nc.vector.tensor_copy(
                wp["scales"][:].bitcast(I32).rearrange("p (t g) -> p g t", t=4),
                wp_sc_raw[:].bitcast(I32).rearrange("p (g t) -> p g t", t=4),
            )

        def p_passes(banks, b):
            for c in range(4):
                js = slice(P * c, P * (c + 1))
                for t in range(4):
                    for a in range(2):
                        at = (t * 4 + a * 2 + b) * P
                        mx(
                            banks[c][:, P * t : P * (t + 1)],
                            wp["words"][:, 2 * at : 2 * (at + P)].bitcast(FP4X4), wp["scales"][:, at : at + P],
                            v_w[a][:, js], v_sc[:, a * S + js.start : a * S + js.stop], a == 0,
                        )

        e32 = [placed("e32_0", 0, [P, 4, S], F32), sb("e32_1", [P, 4, S], F32)]
        e_bf = [sb("e_bf%d" % b, [P, 4 * S], BF16) for b in range(2)]
        q_bf = {}
        e_codes = {1: sb("e_codes1", [P, S], U32)}
        e_sc = [sb("e_sc%d" % b, [P, S], U8) for b in range(2)]
        q_codes = [sb("q_codes%d" % b, [P, S], U32) for b in range(2)]
        q_sc = [sb("q_sc%d" % b, [P, S], U8) for b in range(2)]

        log_gain = sb("log_gain", [P, 2, 4], F32)

        def make_log_gain():
            gain_sb = sb("gain_sb", [P, 2, 4], F32)
            rough = sb("rough", [P, 2, 4], F32)
            inverse = sb("inverse", [P, 2, 4], F32)
            ratio = sb("ratio", [P, 2, 4], F32)
            step = sb("step", [P, 2, 4], F32)
            nc.gpsimd.tensor_copy(gain_sb[:], gain_run[:, :, 0:13:4])
            nc.scalar.activation(rough[:], gain_sb[:], ACT.Ln)
            nc.scalar.activation(inverse[:], rough[:], ACT.Exp, scale=-1.0)
            nc.gpsimd.tensor_tensor(ratio[:], inverse[:], gain_sb[:], ALU.mult)
            nc.gpsimd.tensor_scalar(step[:], ratio[:], 1.0, -1.0, ALU.mult, ALU.add)
            nc.gpsimd.tensor_tensor(log_gain[:], step[:], rough[:], ALU.add)

        def exps(banks, b):
            for t in range(4):
                nc.scalar.activation(e32[b][:, t, :], banks[t][:], ACT.Exp, bias=log_gain[:, b, t : t + 1])

        def round_e(b, js, scalar_share):
            shared_copy(
                e_bf[b][:, 4 * js.start : 4 * js.stop].rearrange("p (c i t) -> p c t i", i=2, t=4),
                e32[b][:, :, js].rearrange("p t (c i) -> p c t i", i=2),
                scalar_share,
            )

        def make_q(banks, b, c):
            nc.vector.tensor_tensor(
                q_bf[b][:, 4 * P * c : 4 * P * (c + 1)].rearrange("p (c i t) -> p c t i", i=2, t=4),
                banks[c][:].rearrange("p (t c i) -> p c t i", t=4, i=2),
                e32[b][:, :, P * c : P * (c + 1)].rearrange("p t (c i) -> p c t i", i=2),
                ALU.mult,
            )

        wf_bf = {}
        wf_codes = [sb("wf_codes%d" % b, [P, N], U32) for b in range(2)]
        wf_sc = [sb("wf_sc%d" % b, [P, N], U8) for b in range(2)]

        def cast_wf(b, engines):
            wf_bf[b] = staged("wf_bf1", "rounded_wf1", [P, 4 * N], BF16) if b else placed("wf_bf0", 0, [P, 4 * N], BF16)
            for w in range(2):
                copy_on(
                    engines[w],
                    wf_bf[b][:].rearrange("p (w u m j) -> p w m j u", w=2, u=2, j=4)[:, w],
                    wf_raw[b][:].rearrange("p j (m w u) -> p w m j u", w=2, u=2)[:, w],
                )

        def quantize_wf(b):
            quantize(wf_codes[b][:], wf_sc[b][:], wf_bf[b][:])

        def second(out, u, codes, scales, js):
            cols = slice(P * u, P * (u + 1))
            for b in range(2):
                mx(out, wf_codes[b][:, cols].bitcast(FP8X4), wf_sc[b][:, cols], codes[b][:, js], scales[b][:, js], b == 0)

        def load_the_rest():
            load_wa(0, 1)
            for r in range(4):
                nc.sync.dma_start(
                    wp_sc_raw[r:P:32, :].bitcast(I32).rearrange("q (a c) -> q a c", a=2),
                    wp_scales.bitcast(I32)[:, r:16:4, :].rearrange("a q c -> q a c"),
                )
            nc.sync.dma_start(wp_w_raw[:], wp_words.bitcast(I32).rearrange("a p c -> p a c"))
            load_wa(1, 0)
            load_wa(1, 1)
            for b in range(2):
                for t in range(4):
                    nc.sync.dma_start(wf_raw[b][:, t, :], wf_view[b, t])
            nc.sync.dma_start(spread_sb[:], spread.rearrange("(p t) -> p t", t=4))

        halves = [slice(0, HALF), slice(HALF, S)]
        for t in range(4):
            cast_wa(0, 0, t, "scalar")
        make_log_gain()
        gather_scales(0)
        gather_scales(1)
        move_scale_rows()
        load_the_rest()
        gather_words(0)
        quantize_wa(0, 0, 0, 4)
        a_banks = [bank(t, "a0_%d" % t) for t in range(4)]
        a_pass(a_banks, 0, 0)
        gather_words(1)
        for t in range(4):
            cast_wa(0, 1, t, "vector" if t < 2 else "scalar")
            quantize_wa(0, 1, t, 1)
        a_pass(a_banks, 0, 1)
        exps(a_banks, 0)
        move_wp_scales()
        move_wp_words()
        for t in range(4):
            cast_wa(1, 0, t, "vector")
        quantize_wa(1, 0, 0, 4)
        for t in range(4):
            cast_wa(1, 1, t, "vector" if t < 3 else "scalar")
            quantize_wa(1, 1, t, 1)
        a_banks = [bank(t, "a1_%d" % t) for t in range(4)]
        a_pass(a_banks, 1, 0)
        a_pass(a_banks, 1, 1)
        exps(a_banks, 1)
        p_banks = [bank(4 + c, "p0_%d" % c) for c in range(4)]
        p_passes(p_banks, 0)
        round_e(0, halves[0], 128)
        round_e(0, halves[1], 128)
        q_bf[0] = staged("q_bf0", "rounded11", [P, 4 * S], BF16)
        for c in range(4):
            make_q(p_banks, 0, c)
        p_banks = [bank(4 + c, "p1_%d" % c) for c in range(4)]
        p_passes(p_banks, 1)
        cast_wf(0, ("vector", "vector"))
        e_codes[0] = placed("e_codes0", 4096, [P, S], U32)
        quantize(e_codes[0][:], e_sc[0][:], e_bf[0][:])
        quantize_wf(0)
        round_e(1, halves[0], 128)
        cast_wf(1, ("scalar", "vector"))
        quantize_wf(1)
        q_bf[1] = staged("q_bf1", "rounded_wf1", [P, 4 * S], BF16)

        root = sb("root", [P, 2, 4, HALF], F32)
        inv_den = sb("inv_den", [P, 2, 4, HALF], F32)
        for h in range(2):
            js = halves[h]
            if h == 1:
                round_e(1, js, 128)
            quantize(e_codes[1][:, js], e_sc[1][:, js], e_bf[1][:, 4 * js.start : 4 * js.stop])
            for k in range(2):
                den = bank(2 * h + k, "den%d%d" % (h, k))
                for u in (2 * k, 2 * k + 1):
                    second(den[:, HALF * (u % 2) : HALF * (u % 2 + 1)], u, e_codes, e_sc, js)
                pair = slice(2 * k, 2 * k + 2)
                nc.scalar.activation(root[:, h, pair, :].rearrange("p u j -> p (u j)"), den[:], ACT.Abs_reciprocal_sqrt)
                nc.scalar.activation(inv_den[:, h, pair, :], root[:, h, pair, :], ACT.Square)
        quantize(q_codes[0][:], q_sc[0][:], q_bf[0][:])

        y_sc = sb("y_sc", [P, S], U8)
        out_rows = out_0.rearrange("(p u) j -> p u j", u=4)
        out_words = out_1[0].rearrange("p m t -> p (m t)").bitcast(I32)
        num_banks = []
        for h in range(2):
            js = slice(HALF * h, HALF * (h + 1))
            make_q(p_banks, 1, 2 * h)
            make_q(p_banks, 1, 2 * h + 1)
            quantize(q_codes[1][:, js], q_sc[1][:, js], q_bf[1][:, 4 * HALF * h : 4 * HALF * (h + 1)])
            pair = [bank(4 + 2 * h + k, "num%d%d" % (h, k)) for k in range(2)]
            num_banks.append(pair)
            for u in range(4):
                second(pair[u // 2][:, HALF * (u % 2) : HALF * (u % 2 + 1)], u, q_codes, q_sc, js)
        for h in range(2):
            js = slice(HALF * h, HALF * (h + 1))
            y32 = sb("y32_%d" % h, [P, 4, HALF], F32)
            y_bf = sb("y_bf%d" % h, [P, 4 * HALF], BF16)
            y_codes = sb("y_codes%d" % h, [P, HALF], U32)
            for u in range(4):
                nc.vector.scalar_tensor_tensor(
                    y32[:, u, :], num_banks[h][u // 2][:, HALF * (u % 2) : HALF * (u % 2 + 1)],
                    spread_sb[:, u : u + 1], inv_den[:, h, u, :], ALU.mult, ALU.mult,
                )
                if h == 1 and u % 2 == 1:
                    nc.sync.dma_start(out_rows[:, u - 1 : u + 1, js], y32[:, u - 1 : u + 1, :])
            if h == 0:
                nc.sync.dma_start(out_rows[:, :, js], y32[:])
            shared_copy(
                y_bf[:].rearrange("p (c i u) -> p c u i", i=2, u=4),
                y32[:].rearrange("p u (c i) -> p c u i", i=2),
                128 if h == 0 else 40,
            )
            quantize(y_codes[:], y_sc[:, js], y_bf[:])
            nc.sync.dma_start(out_words[:, js], y_codes[:].bitcast(I32))
        for r in range(4):
            queue = nc.sync if r % 2 else nc.scalar
            queue.dma_start(out_2[0, r:16:4, :].bitcast(I32), y_sc[r:P:32, :].bitcast(I32))
